import numpy as np
import ml_dtypes


def mxq(x, axis, fmt="e4m3"):
    dtype, down = {"e4m3": (ml_dtypes.float8_e4m3fn, 7), "e5m2": (ml_dtypes.float8_e5m2, 14)}[fmt]
    v = np.moveaxis(np.asarray(x, np.float32).astype(ml_dtypes.bfloat16).astype(np.float64), axis, -1)
    blocks = v.reshape(v.shape[:-1] + (-1, 32))
    amax = np.abs(blocks).max(-1, keepdims=True)
    byte = np.maximum(np.where(amax > 0, np.frexp(amax)[1] - 1 + 127, 0) - down, 1)
    scale = np.exp2(byte - 127.0)
    codes = (blocks / scale).astype(np.float32).astype(dtype).astype(np.float64)
    return np.moveaxis((codes * scale).reshape(v.shape), -1, axis)


WIDE = False


def mx_kscale(k):
    if not WIDE:
        return np.ones(k)
    levels = np.array([10, -10, 5, -5, 0])
    if k % 512:
        return np.exp2(np.random.permutation(np.resize(levels, k // 32))).repeat(32)
    a = np.empty((k // 512, 16))
    for p in range(k // 512):
        a[p, :8] = np.random.permutation(np.resize(levels, 8))
        for g in range(8):
            far = levels[np.abs(levels - a[p, g]) >= 10]
            a[p, g + 8] = far[np.random.randint(len(far))]
    return np.exp2(a.ravel()).repeat(32)


BF16 = ml_dtypes.bfloat16


def bf(x):
    return np.asarray(x, np.float32).astype(BF16)


def f64(x):
    return np.asarray(x).astype(np.float64)

E4M3FN = np.array([(-1.0 if i & 128 else 1.0) * ((1.0 + (i & 7) / 8.0) * 2.0 ** (((i >> 3) & 15) - 7) if i & 120 else (i & 7) * 2.0 ** -9) for i in range(256)])


def e4m3fn_bytes(y):
    return np.clip(np.asarray(y, np.float64), -448.0, 448.0).astype(np.float32).astype(ml_dtypes.float8_e4m3fn).view(np.uint8)


def e4m3fn_values(b):
    return E4M3FN[b]


T, M, D = 2048, 1024, 2048


def setup_inputs():
    s, t = mx_kscale(T), mx_kscale(M)
    snap = np.random.standard_normal((T, M)) + 0.2 * np.random.standard_normal((T, 1)) * np.random.standard_normal((1, M))
    weight = np.random.uniform(0.5, 1.5, (T, 1))
    X = snap * s[:, None]
    X_scale = (np.abs(X).max(axis=1, keepdims=True) / 448).astype(np.float32)
    G = weight * snap / s[:, None] * t
    A = 0.7 * np.random.standard_normal((M, D)) / t[:, None]
    A_scale = (np.abs(A).max(axis=1, keepdims=True) / 448).astype(np.float32)
    return {"X_bytes": e4m3fn_bytes(X / f64(X_scale)),
            "X_scale": X_scale,
            "G": bf(G),
            "load": bf(0.3 * (1 + 0.1 * np.random.standard_normal(M)) * t),
            "A_bytes": e4m3fn_bytes(A / f64(A_scale)),
            "A_scale": A_scale}


def reference(X_bytes, X_scale, G, load, A_bytes, A_scale):
    X = e4m3fn_values(X_bytes) * np.repeat(f64(X_scale), M, axis=1)
    A = e4m3fn_values(A_bytes) * np.repeat(f64(A_scale), D, axis=1)
    C = (mxq(X, 0, "e4m3").T @ mxq(f64(G), 0, "e4m3")) / T
    R = C + np.eye(M) * f64(load)[None, :]
    Z = mxq(R, 1, "e4m3") @ mxq(A, 0, "e4m3")
    return Z

@@ -1,0 +1,193 @@
+from contextlib import ExitStack
+
+import concourse.mybir as mybir
+from concourse.masks import make_identity
+
+T, M, D = 2048, 1024, 2048
+FLOPS = 2 * T * M * M + 2 * M * M * D
+
+F32 = mybir.dt.float32
+BF16 = mybir.dt.bfloat16
+U32 = mybir.dt.uint32
+U8 = mybir.dt.uint8
+FP8 = mybir.dt.float8_e4m3fn
+FP8X4 = mybir.dt.float8_e4m3fn_x4
+COPY = mybir.ActivationFunctionType.Copy
+MULT = mybir.AluOpType.mult
+ADD = mybir.AluOpType.add
+
+P = 128
+W = 512
+KP = 512
+CP = T // KP
+GP = M // KP
+
+
+def tile_loaded_microphone_covariance_d5_kernel(tc, X_bytes, X_scale, G, load, A_bytes, A_scale, out):
+    nc = tc.nc
+    with ExitStack() as ctx:
+        keep = ctx.enter_context(tc.tile_pool(name="keep", bufs=1))
+        stage = ctx.enter_context(tc.tile_pool(name="stage", bufs=4))
+        psum = ctx.enter_context(tc.psum_pool(name="psum", bufs=8))
+
+        xsc = keep.tile([P, CP, 4], F32, name="xsc")
+        nc.scalar.dma_start(out=xsc[:], in_=X_scale.rearrange("(c p t) o -> p c (t o)", p=P, t=4))
+        lb = keep.tile([P, GP, 4], BF16, name="lb")
+        nc.scalar.dma_start(out=lb[:], in_=load.rearrange("(g p t) -> p g t", p=P, t=4))
+        asc = keep.tile([P, GP, 4], F32, name="asc")
+        nc.scalar.dma_start(out=asc[:], in_=A_scale.rearrange("(g p t) o -> p g (t o)", p=P, t=4))
+
+        xv = X_bytes.rearrange("(c p t) w -> c p t w", p=P, t=4)
+        gv = G.rearrange("(c p t) w -> c p t w", p=P, t=4)
+        av = A_bytes.rearrange("(g p t) w -> g p t w", p=P, t=4)
+        x_raw = {}
+        g_raw = {}
+        a_raw = {}
+        for h in range(2):
+            for c in range(CP):
+                if h == 0:
+                    x_raw[c, h] = keep.tile([P, 4, W], U8, name="xraw%d%d" % (c, h))
+                    nc.sync.dma_start(out=x_raw[c, h][:], in_=xv[c][:, :, W * h : W * (h + 1)])
+                g_raw[c, h] = keep.tile([P, 4, W], BF16, name="graw%d%d" % (c, h))
+                nc.sync.dma_start(out=g_raw[c, h][:], in_=gv[c][:, :, W * h : W * (h + 1)])
+        for c in range(CP):
+            x_raw[c, 1] = keep.tile([P, 4, W], U8, name="xraw%d1" % c)
+            nc.sync.dma_start(out=x_raw[c, 1][:], in_=xv[c][:, :, W : 2 * W])
+        for h in range(2):
+            for g in range(GP):
+                a_raw[g, h] = keep.tile([P, 4, 1024], U8, name="araw%d%d" % (g, h))
+                nc.sync.dma_start(out=a_raw[g, h][:], in_=av[g][:, :, 1024 * h : 1024 * (h + 1)])
+
+        ident = keep.tile([P, P], BF16, name="ident")
+        make_identity(nc, ident[:])
+        lf = keep.tile([P, GP * 4], F32, name="lf")
+        nc.scalar.copy(out=lf[:], in_=lb[:].rearrange("p g t -> p (g t)"))
+        diag = {}
+        for g in range(GP):
+            diag[g] = keep.tile([P, W, 4], BF16, name="diag%d" % g)
+            nc.vector.memset(diag[g][:], 0.0)
+            dv = diag[g][:].rearrange("p (q a) t -> p q a t", a=4)
+            for t in range(4):
+                nc.scalar.activation(out=dv[:, :, t, t], in_=ident[:], func=COPY, scale=lf[:, 4 * g + t : 4 * g + t + 1])
+
+        def codes(name):
+            q = keep.tile([P, W], U32, name=name + "q", align_bytes=64)
+            s = keep.tile([P, W], U8, name=name + "s", align_bytes=64)
+            return q, s
+
+        def quantize(qs, grouped):
+            nc.vector.quantize_mx(out=qs[0][:].bitcast(FP8X4), scales=qs[1][:], in_=grouped)
+
+        def widen_and_group(raw, sc, on_vector):
+            wide = stage.tile([P, 4, W], BF16, name="wide", align_bytes=64)
+            for t in range(4):
+                src = raw[:, t].bitcast(FP8)
+                if t in on_vector:
+                    nc.vector.tensor_scalar(out=wide[:, t], in0=src, scalar1=sc[:, t : t + 1], scalar2=None, op0=MULT)
+                else:
+                    nc.scalar.activation(out=wide[:, t], in_=src, func=COPY, scale=sc[:, t : t + 1])
+            grouped = stage.tile([P, W, 4], BF16, name="grouped", align_bytes=64)
+            nc.vector.tensor_copy(
+                out=grouped[:].rearrange("p (c i) t -> p c t i", i=4),
+                in_=wide[:].rearrange("p t (c i) -> p c t i", i=4),
+            )
+            return grouped[:].rearrange("p w t -> p (w t)")
+
+        xq = {}
+        gq = {}
+        aq = {}
+        rq = {}
+
+        def x_unit(c, h, on_vector):
+            xq[c, h] = codes("x%d%d" % (c, h))
+            quantize(xq[c, h], widen_and_group(x_raw[c, h][:], xsc[:, c], on_vector))
+
+        def g_unit(c, g):
+            gq[c, g] = codes("g%d%d" % (c, g))
+            gg = stage.tile([P, 4 * W], BF16, name="gg", align_bytes=64)
+            src = g_raw[c, g][:].rearrange("p j (m t) -> p t m j", t=4)
+            for b in range(2):
+                pg = psum.tile([P, 1024], BF16, name="bank")
+                for k in range(2):
+                    nc.tensor.matmul(
+                        out=pg[:, 512 * k : 512 * (k + 1)].rearrange("p (m j) -> p m j", j=4),
+                        lhsT=ident[:],
+                        rhs=src[:, 2 * b + k],
+                        start=True,
+                        stop=True,
+                    )
+                nc.scalar.copy(out=gg[:, 1024 * b : 1024 * (b + 1)], in_=pg[:])
+            quantize(gq[c, g], gg[:])
+
+        def c_block(h, g):
+            rq[h, g] = codes("r%d%d" % (h, g))
+            rg = stage.tile([P, W, 4], BF16, name="rg", align_bytes=64)
+            for b in range(4):
+                acc = psum.tile([P, 4, P], F32, name="bank")
+                for t in range(4):
+                    for c in range(CP):
+                        nc.tensor.matmul_mx(
+                            out=acc[:, t],
+                            lhsT=gq[c, g][0][:, P * t : P * (t + 1)].bitcast(FP8X4),
+                            lhsT_scale=gq[c, g][1][:, P * t : P * (t + 1)],
+                            rhs=xq[c, h][0][:, P * b : P * (b + 1)].bitcast(FP8X4),
+                            rhs_scale=xq[c, h][1][:, P * b : P * (b + 1)],
+                            start=(c == 0),
+                            stop=(c == CP - 1),
+                        )
+                src = acc[:].rearrange("p t i -> p i t")
+                dst = rg[:, P * b : P * (b + 1)]
+                if h == g:
+                    nc.vector.scalar_tensor_tensor(
+                        out=dst, in0=src, scalar=1.0 / T, in1=diag[g][:, P * b : P * (b + 1)], op0=MULT, op1=ADD
+                    )
+                else:
+                    nc.scalar.activation(out=dst, in_=src, func=COPY, scale=1.0 / T)
+            quantize(rq[h, g], rg[:].rearrange("p w t -> p (w t)"))
+
+        def a_unit(d, g, on_vector):
+            aq[d, g] = codes("a%d%d" % (d, g))
+            raw = a_raw[g, d // 2][:, :, W * (d % 2) : W * (d % 2 + 1)]
+            quantize(aq[d, g], widen_and_group(raw, asc[:, g], on_vector))
+
+        def z_block(h, d):
+            for b in range(4):
+                acc = psum.tile([P, W], F32, name="bank")
+                for g in range(GP):
+                    nc.tensor.matmul_mx(
+                        out=acc[:],
+                        lhsT=rq[h, g][0][:, P * b : P * (b + 1)].bitcast(FP8X4),
+                        lhsT_scale=rq[h, g][1][:, P * b : P * (b + 1)],
+                        rhs=aq[d, g][0][:].bitcast(FP8X4),
+                        rhs_scale=aq[d, g][1][:],
+                        start=(g == 0),
+                        stop=(g == GP - 1),
+                    )
+                zt = stage.tile([P, W], F32, name="zt", bufs=8)
+                if b % 2 == 1 and d == 3 and h == 1:
+                    nc.vector.tensor_copy(out=zt[:], in_=acc[:])
+                else:
+                    nc.scalar.copy(out=zt[:], in_=acc[:])
+                row = W * h + P * b
+                nc.sync.dma_start(out=out[row : row + P, W * d : W * (d + 1)], in_=zt[:])
+
+        for c in range(CP):
+            x_unit(c, 0, (0,))
+            g_unit(c, 0)
+        for c in range(CP):
+            g_unit(c, 1)
+        c_block(0, 0)
+        c_block(0, 1)
+        for c in range(CP):
+            x_unit(c, 1, (0,))
+        a_unit(0, 0, (0, 1))
+        a_unit(0, 1, (0, 1))
+        z_block(0, 0)
+        c_block(1, 0)
+        c_block(1, 1)
+        z_block(1, 0)
+        for d in range(1, 4):
+            for g in range(GP):
+                a_unit(d, g, (0, 1, 2))
+            z_block(0, d)
+            z_block(1, d)

@@ -105,18 +105,10 @@ def tile_loaded_microphone_covariance_d5_kernel(tc, X_bytes, X_scale, G, load, A
         def g_unit(c, g):
             gq[c, g] = codes("g%d%d" % (c, g))
             gg = stage.tile([P, 4 * W], BF16, name="gg", align_bytes=64)
-            src = g_raw[c, g][:].rearrange("p j (m t) -> p t m j", t=4)
-            for b in range(2):
-                pg = psum.tile([P, 1024], BF16, name="bank")
-                for k in range(2):
-                    nc.tensor.matmul(
-                        out=pg[:, 512 * k : 512 * (k + 1)].rearrange("p (m j) -> p m j", j=4),
-                        lhsT=ident[:],
-                        rhs=src[:, 2 * b + k],
-                        start=True,
-                        stop=True,
-                    )
-                nc.scalar.copy(out=gg[:, 1024 * b : 1024 * (b + 1)], in_=pg[:])
+            nc.vector.tensor_copy(
+                out=gg[:].rearrange("p (t m j) -> p m j t", t=4, j=4),
+                in_=g_raw[c, g][:].rearrange("p j (m t) -> p m j t", t=4),
+            )
             quantize(gq[c, g], gg[:])
 
         def c_block(h, g):
@@ -172,22 +164,22 @@ def tile_loaded_microphone_covariance_d5_kernel(tc, X_bytes, X_scale, G, load, A
                 nc.sync.dma_start(out=out[row : row + P, W * d : W * (d + 1)], in_=zt[:])
 
         for c in range(CP):
-            x_unit(c, 0, (0,))
+            x_unit(c, 0, ())
             g_unit(c, 0)
         for c in range(CP):
             g_unit(c, 1)
         c_block(0, 0)
         c_block(0, 1)
         for c in range(CP):
-            x_unit(c, 1, (0,))
-        a_unit(0, 0, (0, 1))
-        a_unit(0, 1, (0, 1))
+            x_unit(c, 1, ())
+        a_unit(0, 0, (0,))
+        a_unit(0, 1, (0,))
         z_block(0, 0)
         c_block(1, 0)
         c_block(1, 1)
         z_block(1, 0)
         for d in range(1, 4):
             for g in range(GP):
-                a_unit(d, g, (0, 1, 2))
+                a_unit(d, g, (0, 1))
             z_block(0, d)
             z_block(1, d)

@@ -43,16 +43,17 @@ def tile_loaded_microphone_covariance_d5_kernel(tc, X_bytes, X_scale, G, load, A
         x_raw = {}
         g_raw = {}
         a_raw = {}
-        for h in range(2):
-            for c in range(CP):
-                if h == 0:
-                    x_raw[c, h] = keep.tile([P, 4, W], U8, name="xraw%d%d" % (c, h))
-                    nc.sync.dma_start(out=x_raw[c, h][:], in_=xv[c][:, :, W * h : W * (h + 1)])
-                g_raw[c, h] = keep.tile([P, 4, W], BF16, name="graw%d%d" % (c, h))
-                nc.sync.dma_start(out=g_raw[c, h][:], in_=gv[c][:, :, W * h : W * (h + 1)])
+        for c in range(CP):
+            x_raw[c, 0] = keep.tile([P, 4, W], U8, name="xraw%d0" % c)
+            nc.sync.dma_start(out=x_raw[c, 0][:], in_=xv[c][:, :, 0:W])
+            g_raw[c, 0] = keep.tile([P, 4, W], BF16, name="graw%d0" % c)
+            nc.sync.dma_start(out=g_raw[c, 0][:], in_=gv[c][:, :, 0:W])
         for c in range(CP):
             x_raw[c, 1] = keep.tile([P, 4, W], U8, name="xraw%d1" % c)
             nc.sync.dma_start(out=x_raw[c, 1][:], in_=xv[c][:, :, W : 2 * W])
+        for c in range(CP):
+            g_raw[c, 1] = keep.tile([P, 4, W], BF16, name="graw%d1" % c)
+            nc.sync.dma_start(out=g_raw[c, 1][:], in_=gv[c][:, :, W : 2 * W])
         for h in range(2):
             for g in range(GP):
                 a_raw[g, h] = keep.tile([P, 4, 1024], U8, name="araw%d%d" % (g, h))
@@ -60,126 +61,222 @@ def tile_loaded_microphone_covariance_d5_kernel(tc, X_bytes, X_scale, G, load, A
 
         ident = keep.tile([P, P], BF16, name="ident")
         make_identity(nc, ident[:])
-        lf = keep.tile([P, GP * 4], F32, name="lf")
-        nc.scalar.copy(out=lf[:], in_=lb[:].rearrange("p g t -> p (g t)"))
         diag = {}
         for g in range(GP):
             diag[g] = keep.tile([P, W, 4], BF16, name="diag%d" % g)
             nc.vector.memset(diag[g][:], 0.0)
-            dv = diag[g][:].rearrange("p (q a) t -> p q a t", a=4)
-            for t in range(4):
-                nc.scalar.activation(out=dv[:, :, t, t], in_=ident[:], func=COPY, scale=lf[:, 4 * g + t : 4 * g + t + 1])
+            nc.gpsimd.tensor_tensor(
+                out=diag[g][:].rearrange("p (q a) t -> p q (a t)", a=4)[:, :, 0:16:5],
+                in0=ident[:].unsqueeze(2).to_broadcast([P, P, 4]),
+                in1=lb[:, g : g + 1, :].to_broadcast([P, P, 4]),
+                op=MULT,
+            )
 
         def codes(name):
             q = keep.tile([P, W], U32, name=name + "q", align_bytes=64)
             s = keep.tile([P, W], U8, name=name + "s", align_bytes=64)
             return q, s
 
-        def quantize(qs, grouped):
-            nc.vector.quantize_mx(out=qs[0][:].bitcast(FP8X4), scales=qs[1][:], in_=grouped)
+        wide = {}
+        grouped = {}
+        coded = {}
+        bank = {}
+        rows = {}
 
-        def widen_and_group(raw, sc, on_vector):
-            wide = stage.tile([P, 4, W], BF16, name="wide", align_bytes=64)
+        def source(u):
+            if u[0] == "x":
+                return x_raw[u[1], u[2]][:], xsc[:, u[1]]
+            raw = a_raw[u[2], u[1] // 2][:, :, W * (u[1] % 2) : W * (u[1] % 2 + 1)]
+            return raw, asc[:, u[2]]
+
+        def widen(u, on_vector):
+            raw, sc = source(u)
+            wt = stage.tile([P, 4, W], BF16, name="wide", align_bytes=64, bufs=6)
+            wide[u] = wt
             for t in range(4):
                 src = raw[:, t].bitcast(FP8)
-                if t in on_vector:
-                    nc.vector.tensor_scalar(out=wide[:, t], in0=src, scalar1=sc[:, t : t + 1], scalar2=None, op0=MULT)
+                if t < on_vector:
+                    nc.vector.tensor_scalar(out=wt[:, t], in0=src, scalar1=sc[:, t : t + 1], scalar2=None, op0=MULT)
                 else:
-                    nc.scalar.activation(out=wide[:, t], in_=src, func=COPY, scale=sc[:, t : t + 1])
-            grouped = stage.tile([P, W, 4], BF16, name="grouped", align_bytes=64)
-            nc.vector.tensor_copy(
-                out=grouped[:].rearrange("p (c i) t -> p c t i", i=4),
-                in_=wide[:].rearrange("p t (c i) -> p c t i", i=4),
+                    nc.scalar.activation(out=wt[:, t], in_=src, func=COPY, scale=sc[:, t : t + 1])
+
+        def group(u, eng):
+            gt = stage.tile([P, 4 * W], BF16, name="grouped", align_bytes=64, bufs=6)
+            grouped[u] = gt
+            if u[0] == "g":
+                dst = gt[:].rearrange("p (t m j) -> p m j t", t=4, j=4)
+                src = g_raw[u[1], u[2]][:].rearrange("p j (m t) -> p m j t", t=4)
+            else:
+                dst = gt[:].rearrange("p (c i t) -> p c t i", i=4, t=4)
+                src = wide[u][:].rearrange("p t (c i) -> p c t i", i=4)
+            if eng is nc.scalar:
+                nc.scalar.copy(out=dst, in_=src)
+            else:
+                nc.vector.tensor_copy(out=dst, in_=src)
+
+        def quantize(qs, src):
+            nc.vector.quantize_mx(out=qs[0][:].bitcast(FP8X4), scales=qs[1][:], in_=src)
+
+        def quant(u):
+            coded[u] = codes("%s%d%d" % u)
+            quantize(coded[u], grouped[u][:])
+
+        def mx(acc, left, lcols, right, rcols, first, last):
+            nc.tensor.matmul_mx(
+                out=acc,
+                lhsT=left[0][:, lcols].bitcast(FP8X4),
+                lhsT_scale=left[1][:, lcols],
+                rhs=right[0][:, rcols].bitcast(FP8X4),
+                rhs_scale=right[1][:, rcols],
+                start=first,
+                stop=last,
             )
-            return grouped[:].rearrange("p w t -> p (w t)")
 
-        xq = {}
-        gq = {}
-        aq = {}
-        rq = {}
-
-        def x_unit(c, h, on_vector):
-            xq[c, h] = codes("x%d%d" % (c, h))
-            quantize(xq[c, h], widen_and_group(x_raw[c, h][:], xsc[:, c], on_vector))
-
-        def g_unit(c, g):
-            gq[c, g] = codes("g%d%d" % (c, g))
-            gg = stage.tile([P, 4 * W], BF16, name="gg", align_bytes=64)
-            nc.vector.tensor_copy(
-                out=gg[:].rearrange("p (t m j) -> p m j t", t=4, j=4),
-                in_=g_raw[c, g][:].rearrange("p j (m t) -> p m j t", t=4),
-            )
-            quantize(gq[c, g], gg[:])
-
-        def c_block(h, g):
-            rq[h, g] = codes("r%d%d" % (h, g))
-            rg = stage.tile([P, W, 4], BF16, name="rg", align_bytes=64)
+        def c_mm(h, g):
             for b in range(4):
                 acc = psum.tile([P, 4, P], F32, name="bank")
+                bank["c", h, g, b] = acc
                 for t in range(4):
                     for c in range(CP):
-                        nc.tensor.matmul_mx(
-                            out=acc[:, t],
-                            lhsT=gq[c, g][0][:, P * t : P * (t + 1)].bitcast(FP8X4),
-                            lhsT_scale=gq[c, g][1][:, P * t : P * (t + 1)],
-                            rhs=xq[c, h][0][:, P * b : P * (b + 1)].bitcast(FP8X4),
-                            rhs_scale=xq[c, h][1][:, P * b : P * (b + 1)],
-                            start=(c == 0),
-                            stop=(c == CP - 1),
-                        )
-                src = acc[:].rearrange("p t i -> p i t")
-                dst = rg[:, P * b : P * (b + 1)]
+                        mx(acc[:, t], coded["g", c, g], slice(P * t, P * (t + 1)), coded["x", c, h], slice(P * b, P * (b + 1)), c == 0, c == CP - 1)
+
+        def c_out(h, g, half):
+            if half == 0:
+                rows[h, g] = stage.tile([P, W, 4], BF16, name="rows", align_bytes=64, bufs=3)
+            for b in (2 * half, 2 * half + 1):
+                src = bank["c", h, g, b][:].rearrange("p t i -> p i t")
+                dst = rows[h, g][:, P * b : P * (b + 1)]
                 if h == g:
                     nc.vector.scalar_tensor_tensor(
                         out=dst, in0=src, scalar=1.0 / T, in1=diag[g][:, P * b : P * (b + 1)], op0=MULT, op1=ADD
                     )
                 else:
                     nc.scalar.activation(out=dst, in_=src, func=COPY, scale=1.0 / T)
-            quantize(rq[h, g], rg[:].rearrange("p w t -> p (w t)"))
 
-        def a_unit(d, g, on_vector):
-            aq[d, g] = codes("a%d%d" % (d, g))
-            raw = a_raw[g, d // 2][:, :, W * (d % 2) : W * (d % 2 + 1)]
-            quantize(aq[d, g], widen_and_group(raw, asc[:, g], on_vector))
+        def r_quant(h, g):
+            coded["r", h, g] = codes("r%d%d" % (h, g))
+            quantize(coded["r", h, g], rows[h, g][:].rearrange("p w t -> p (w t)"))
 
-        def z_block(h, d):
+        def z_mm(h, d):
             for b in range(4):
                 acc = psum.tile([P, W], F32, name="bank")
+                bank["z", h, d, b] = acc
                 for g in range(GP):
-                    nc.tensor.matmul_mx(
-                        out=acc[:],
-                        lhsT=rq[h, g][0][:, P * b : P * (b + 1)].bitcast(FP8X4),
-                        lhsT_scale=rq[h, g][1][:, P * b : P * (b + 1)],
-                        rhs=aq[d, g][0][:].bitcast(FP8X4),
-                        rhs_scale=aq[d, g][1][:],
-                        start=(g == 0),
-                        stop=(g == GP - 1),
-                    )
+                    mx(acc[:], coded["r", h, g], slice(P * b, P * (b + 1)), coded["a", d, g], slice(0, W), g == 0, g == GP - 1)
+
+        def z_out(h, d, half, on_vector):
+            for k in range(2):
+                b = 2 * half + k
                 zt = stage.tile([P, W], F32, name="zt", bufs=8)
-                if b % 2 == 1 and d == 3 and h == 1:
-                    nc.vector.tensor_copy(out=zt[:], in_=acc[:])
+                if k < on_vector:
+                    nc.vector.tensor_copy(out=zt[:], in_=bank["z", h, d, b][:])
                 else:
-                    nc.scalar.copy(out=zt[:], in_=acc[:])
+                    nc.scalar.copy(out=zt[:], in_=bank["z", h, d, b][:])
                 row = W * h + P * b
                 nc.sync.dma_start(out=out[row : row + P, W * d : W * (d + 1)], in_=zt[:])
 
-        for c in range(CP):
-            x_unit(c, 0, ())
-            g_unit(c, 0)
-        for c in range(CP):
-            g_unit(c, 1)
-        c_block(0, 0)
-        c_block(0, 1)
-        for c in range(CP):
-            x_unit(c, 1, ())
-        a_unit(0, 0, (0,))
-        a_unit(0, 1, (0,))
-        z_block(0, 0)
-        c_block(1, 0)
-        c_block(1, 1)
-        z_block(1, 0)
-        for d in range(1, 4):
-            for g in range(GP):
-                a_unit(d, g, (0, 1))
-            z_block(0, d)
-            z_block(1, d)
+        with tc.manual_schedule():
+            widen(('x', 0, 0), 3)
+            group(('x', 0, 0), nc.vector)
+            group(('g', 0, 0), nc.scalar)
+            widen(('x', 1, 0), 3)
+            quant(('x', 0, 0))
+            widen(('x', 2, 0), 0)
+            group(('g', 1, 0), nc.vector)
+            quant(('g', 0, 0))
+            group(('g', 2, 0), nc.scalar)
+            group(('x', 1, 0), nc.vector)
+            widen(('x', 3, 0), 2)
+            quant(('g', 1, 0))
+            group(('x', 2, 0), nc.vector)
+            widen(('x', 0, 1), 4)
+            quant(('g', 2, 0))
+            quant(('x', 2, 0))
+            widen(('x', 2, 1), 2)
+            widen(('x', 3, 1), 3)
+            group(('x', 3, 0), nc.vector)
+            group(('g', 3, 0), nc.scalar)
+            group(('g', 1, 1), nc.scalar)
+            group(('g', 3, 1), nc.scalar)
+            quant(('x', 1, 0))
+            group(('g', 0, 1), nc.vector)
+            quant(('x', 3, 0))
+            quant(('g', 3, 0))
+            group(('g', 2, 1), nc.scalar)
+            quant(('g', 1, 1))
+            widen(('x', 1, 1), 0)
+            group(('x', 3, 1), nc.vector)
+            c_mm(0, 0)
+            quant(('g', 0, 1))
+            group(('x', 2, 1), nc.vector)
+            quant(('g', 3, 1))
+            widen(('a', 0, 1), 0)
+            group(('x', 0, 1), nc.vector)
+            widen(('a', 1, 0), 0)
+            quant(('g', 2, 1))
+            quant(('x', 3, 1))
+            quant(('x', 2, 1))
+            c_out(0, 0, 0)
+            group(('x', 1, 1), nc.vector)
+            quant(('x', 0, 1))
+            quant(('x', 1, 1))
+            c_out(0, 0, 1)
+            c_mm(0, 1)
+            widen(('a', 0, 0), 1)
+            c_out(0, 1, 0)
+            r_quant(0, 0)
+            group(('a', 0, 1), nc.vector)
+            group(('a', 1, 0), nc.vector)
+            group(('a', 0, 0), nc.vector)
+            widen(('a', 1, 1), 1)
+            c_out(0, 1, 1)
+            quant(('a', 0, 0))
+            c_mm(1, 0)
+            quant(('a', 1, 0))
+            c_mm(1, 1)
+            group(('a', 1, 1), nc.vector)
+            widen(('a', 3, 0), 0)
+            quant(('a', 0, 1))
+            r_quant(0, 1)
+            c_out(1, 0, 0)
+            c_out(1, 1, 0)
+            quant(('a', 1, 1))
+            c_out(1, 0, 1)
+            c_out(1, 1, 1)
+            r_quant(1, 0)
+            r_quant(1, 1)
+            widen(('a', 2, 1), 2)
+            z_mm(0, 0)
+            z_mm(0, 1)
+            z_out(0, 0, 0, 0)
+            z_out(0, 0, 1, 0)
+            widen(('a', 2, 0), 4)
+            group(('a', 2, 1), nc.vector)
+            group(('a', 2, 0), nc.vector)
+            z_out(0, 1, 0, 0)
+            quant(('a', 2, 1))
+            z_out(0, 1, 1, 0)
+            z_mm(1, 0)
+            z_mm(1, 1)
+            z_out(1, 0, 0, 0)
+            z_out(1, 0, 1, 0)
+            z_out(1, 1, 0, 0)
+            z_out(1, 1, 1, 0)
+            quant(('a', 2, 0))
+            widen(('a', 3, 1), 4)
+            group(('a', 3, 0), nc.vector)
+            z_mm(0, 2)
+            z_out(0, 2, 0, 0)
+            z_out(0, 2, 1, 0)
+            group(('a', 3, 1), nc.vector)
+            z_mm(1, 2)
+            quant(('a', 3, 0))
+            z_out(1, 2, 0, 0)
+            z_out(1, 2, 1, 0)
+            quant(('a', 3, 1))
+            z_mm(0, 3)
+            z_out(0, 3, 1, 0)
+            z_out(0, 3, 0, 2)
+            z_mm(1, 3)
+            z_out(1, 3, 0, 2)
+            z_out(1, 3, 1, 2)

@@ -21,19 +21,20 @@ W = 512
 KP = 512
 CP = T // KP
 GP = M // KP
+A_COLS = ((0, 512), (512, 512), (1024, 512), (1536, 256), (1792, 256))
 
 
 def tile_loaded_microphone_covariance_d5_kernel(tc, X_bytes, X_scale, G, load, A_bytes, A_scale, out):
     nc = tc.nc
     with ExitStack() as ctx:
         keep = ctx.enter_context(tc.tile_pool(name="keep", bufs=1))
-        stage = ctx.enter_context(tc.tile_pool(name="stage", bufs=4))
+        stage = ctx.enter_context(tc.tile_pool(name="stage", bufs=1))
         psum = ctx.enter_context(tc.psum_pool(name="psum", bufs=8))
 
-        xsc = keep.tile([P, CP, 4], F32, name="xsc")
-        nc.scalar.dma_start(out=xsc[:], in_=X_scale.rearrange("(c p t) o -> p c (t o)", p=P, t=4))
         lb = keep.tile([P, GP, 4], BF16, name="lb")
         nc.scalar.dma_start(out=lb[:], in_=load.rearrange("(g p t) -> p g t", p=P, t=4))
+        xsc = keep.tile([P, CP, 4], F32, name="xsc")
+        nc.scalar.dma_start(out=xsc[:], in_=X_scale.rearrange("(c p t) o -> p c (t o)", p=P, t=4))
         asc = keep.tile([P, GP, 4], F32, name="asc")
         nc.scalar.dma_start(out=asc[:], in_=A_scale.rearrange("(g p t) o -> p g (t o)", p=P, t=4))
 
@@ -43,17 +44,24 @@ def tile_loaded_microphone_covariance_d5_kernel(tc, X_bytes, X_scale, G, load, A
         x_raw = {}
         g_raw = {}
         a_raw = {}
+
+        def load_x(c, h):
+            x_raw[c, h] = keep.tile([P, 4, W], U8, name="xraw%d%d" % (c, h))
+            cuts = (0, 2, 4) if c == 0 and h == 0 else (0, 4)
+            for lo, hi in zip(cuts, cuts[1:]):
+                nc.sync.dma_start(out=x_raw[c, h][:, lo:hi], in_=xv[c][:, lo:hi, W * h : W * (h + 1)])
+
+        def load_g(c, h):
+            g_raw[c, h] = stage.tile([P, 4, W], BF16, name="graw%d%d" % (c, h), tag="stream", bufs=8)
+            nc.sync.dma_start(out=g_raw[c, h][:], in_=gv[c][:, :, W * h : W * (h + 1)])
+
         for c in range(CP):
-            x_raw[c, 0] = keep.tile([P, 4, W], U8, name="xraw%d0" % c)
-            nc.sync.dma_start(out=x_raw[c, 0][:], in_=xv[c][:, :, 0:W])
-            g_raw[c, 0] = keep.tile([P, 4, W], BF16, name="graw%d0" % c)
-            nc.sync.dma_start(out=g_raw[c, 0][:], in_=gv[c][:, :, 0:W])
+            load_x(c, 0)
+            load_g(c, 0)
         for c in range(CP):
-            x_raw[c, 1] = keep.tile([P, 4, W], U8, name="xraw%d1" % c)
-            nc.sync.dma_start(out=x_raw[c, 1][:], in_=xv[c][:, :, W : 2 * W])
+            load_x(c, 1)
         for c in range(CP):
-            g_raw[c, 1] = keep.tile([P, 4, W], BF16, name="graw%d1" % c)
-            nc.sync.dma_start(out=g_raw[c, 1][:], in_=gv[c][:, :, W : 2 * W])
+            load_g(c, 1)
         for h in range(2):
             for g in range(GP):
                 a_raw[g, h] = keep.tile([P, 4, 1024], U8, name="araw%d%d" % (g, h))
@@ -62,19 +70,20 @@ def tile_loaded_microphone_covariance_d5_kernel(tc, X_bytes, X_scale, G, load, A
         ident = keep.tile([P, P], BF16, name="ident")
         make_identity(nc, ident[:])
         diag = {}
-        for g in range(GP):
+
+        def make_diag(g):
             diag[g] = keep.tile([P, W, 4], BF16, name="diag%d" % g)
             nc.vector.memset(diag[g][:], 0.0)
-            nc.gpsimd.tensor_tensor(
+            nc.vector.tensor_tensor(
                 out=diag[g][:].rearrange("p (q a) t -> p q (a t)", a=4)[:, :, 0:16:5],
                 in0=ident[:].unsqueeze(2).to_broadcast([P, P, 4]),
                 in1=lb[:, g : g + 1, :].to_broadcast([P, P, 4]),
                 op=MULT,
             )
 
-        def codes(name):
-            q = keep.tile([P, W], U32, name=name + "q", align_bytes=64)
-            s = keep.tile([P, W], U8, name=name + "s", align_bytes=64)
+        def codes(name, width):
+            q = keep.tile([P, width], U32, name=name + "q", align_bytes=64)
+            s = keep.tile([P, width], U8, name=name + "s", align_bytes=64)
             return q, s
 
         wide = {}
@@ -83,65 +92,69 @@ def tile_loaded_microphone_covariance_d5_kernel(tc, X_bytes, X_scale, G, load, A
         bank = {}
         rows = {}
 
-        def source(u):
+        def width_of(u):
+            return A_COLS[u[1]][1] if u[0] == "a" else W
+
+        def bytes_of(u):
             if u[0] == "x":
                 return x_raw[u[1], u[2]][:], xsc[:, u[1]]
-            raw = a_raw[u[2], u[1] // 2][:, :, W * (u[1] % 2) : W * (u[1] % 2 + 1)]
-            return raw, asc[:, u[2]]
+            lo, w = A_COLS[u[1]]
+            return a_raw[u[2], lo // 1024][:, :, lo % 1024 : lo % 1024 + w], asc[:, u[2]]
 
-        def widen(u, on_vector):
-            raw, sc = source(u)
-            wt = stage.tile([P, 4, W], BF16, name="wide", align_bytes=64, bufs=6)
-            wide[u] = wt
-            for t in range(4):
-                src = raw[:, t].bitcast(FP8)
-                if t < on_vector:
-                    nc.vector.tensor_scalar(out=wt[:, t], in0=src, scalar1=sc[:, t : t + 1], scalar2=None, op0=MULT)
+        def widen(u, planes, on_scalar):
+            raw, sc = bytes_of(u)
+            if u not in wide:
+                wide[u] = stage.tile([P, 4, width_of(u)], BF16, name="wide", align_bytes=64, bufs=6)
+            for t in planes:
+                dst, src = wide[u][:, t], raw[:, t].bitcast(FP8)
+                if on_scalar:
+                    nc.scalar.activation(out=dst, in_=src, func=COPY, scale=sc[:, t : t + 1])
                 else:
-                    nc.scalar.activation(out=wt[:, t], in_=src, func=COPY, scale=sc[:, t : t + 1])
+                    nc.vector.tensor_scalar(out=dst, in0=src, scalar1=sc[:, t : t + 1], scalar2=None, op0=MULT)
 
-        def group(u, eng):
-            gt = stage.tile([P, 4 * W], BF16, name="grouped", align_bytes=64, bufs=6)
-            grouped[u] = gt
+        def group(u, on_scalar):
+            grouped[u] = stage.tile([P, 4 * width_of(u)], BF16, name="grouped", align_bytes=64, bufs=6)
+            gt = grouped[u][:]
             if u[0] == "g":
-                dst = gt[:].rearrange("p (t m j) -> p m j t", t=4, j=4)
+                dst = gt.rearrange("p (t m j) -> p m j t", t=4, j=4)
                 src = g_raw[u[1], u[2]][:].rearrange("p j (m t) -> p m j t", t=4)
             else:
-                dst = gt[:].rearrange("p (c i t) -> p c t i", i=4, t=4)
+                dst = gt.rearrange("p (c i t) -> p c t i", i=4, t=4)
                 src = wide[u][:].rearrange("p t (c i) -> p c t i", i=4)
-            if eng is nc.scalar:
+            if on_scalar:
                 nc.scalar.copy(out=dst, in_=src)
             else:
                 nc.vector.tensor_copy(out=dst, in_=src)
 
-        def quantize(qs, src):
-            nc.vector.quantize_mx(out=qs[0][:].bitcast(FP8X4), scales=qs[1][:], in_=src)
+        def quantize(key, src, width):
+            q, s = codes("%s%d%d" % key, width)
+            coded[key] = q, s
+            nc.vector.quantize_mx(out=q[:].bitcast(FP8X4), scales=s[:], in_=src)
 
         def quant(u):
-            coded[u] = codes("%s%d%d" % u)
-            quantize(coded[u], grouped[u][:])
+            quantize(u, grouped[u][:], width_of(u))
 
-        def mx(acc, left, lcols, right, rcols, first, last):
+        def mx(acc, left, lcol, right, rcol, n, first, last):
             nc.tensor.matmul_mx(
                 out=acc,
-                lhsT=left[0][:, lcols].bitcast(FP8X4),
-                lhsT_scale=left[1][:, lcols],
-                rhs=right[0][:, rcols].bitcast(FP8X4),
-                rhs_scale=right[1][:, rcols],
+                lhsT=left[0][:, lcol : lcol + P].bitcast(FP8X4),
+                lhsT_scale=left[1][:, lcol : lcol + P],
+                rhs=right[0][:, rcol : rcol + n].bitcast(FP8X4),
+                rhs_scale=right[1][:, rcol : rcol + n],
                 start=first,
                 stop=last,
             )
 
-        def c_mm(h, g):
-            for b in range(4):
+        def c_mm(h, g, half):
+            for b in (2 * half, 2 * half + 1):
                 acc = psum.tile([P, 4, P], F32, name="bank")
                 bank["c", h, g, b] = acc
                 for t in range(4):
                     for c in range(CP):
-                        mx(acc[:, t], coded["g", c, g], slice(P * t, P * (t + 1)), coded["x", c, h], slice(P * b, P * (b + 1)), c == 0, c == CP - 1)
+                        mx(acc[:, t], coded["g", c, g], P * t, coded["x", c, h], P * b, P, c == 0, c == CP - 1)
 
         def c_out(h, g, half):
-            if half == 0:
+            if (h, g) not in rows:
                 rows[h, g] = stage.tile([P, W, 4], BF16, name="rows", align_bytes=64, bufs=3)
             for b in (2 * half, 2 * half + 1):
                 src = bank["c", h, g, b][:].rearrange("p t i -> p i t")
@@ -154,129 +167,161 @@ def tile_loaded_microphone_covariance_d5_kernel(tc, X_bytes, X_scale, G, load, A
                     nc.scalar.activation(out=dst, in_=src, func=COPY, scale=1.0 / T)
 
         def r_quant(h, g):
-            coded["r", h, g] = codes("r%d%d" % (h, g))
-            quantize(coded["r", h, g], rows[h, g][:].rearrange("p w t -> p (w t)"))
+            quantize(("r", h, g), rows[h, g][:].rearrange("p w t -> p (w t)"), W)
 
-        def z_mm(h, d):
-            for b in range(4):
-                acc = psum.tile([P, W], F32, name="bank")
+        def z_mm(h, d, half):
+            w = A_COLS[d][1]
+            for b in (2 * half, 2 * half + 1):
+                acc = psum.tile([P, w], F32, name="bank")
                 bank["z", h, d, b] = acc
                 for g in range(GP):
-                    mx(acc[:], coded["r", h, g], slice(P * b, P * (b + 1)), coded["a", d, g], slice(0, W), g == 0, g == GP - 1)
+                    mx(acc[:], coded["r", h, g], P * b, coded["a", d, g], 0, w, g == 0, g == GP - 1)
 
         def z_out(h, d, half, on_vector):
+            lo, w = A_COLS[d]
+            zt = stage.tile([P, 2, w], F32, name="zt", tag="stream", bufs=8)
             for k in range(2):
-                b = 2 * half + k
-                zt = stage.tile([P, W], F32, name="zt", bufs=8)
+                src = bank["z", h, d, 2 * half + k]
                 if k < on_vector:
-                    nc.vector.tensor_copy(out=zt[:], in_=bank["z", h, d, b][:])
+                    nc.vector.tensor_copy(out=zt[:, k], in_=src[:])
                 else:
-                    nc.scalar.copy(out=zt[:], in_=bank["z", h, d, b][:])
-                row = W * h + P * b
-                nc.sync.dma_start(out=out[row : row + P, W * d : W * (d + 1)], in_=zt[:])
+                    nc.scalar.copy(out=zt[:, k], in_=src[:])
+            row = W * h + 2 * P * half
+            nc.sync.dma_start(out=out[row : row + 2 * P, lo : lo + w].rearrange("(k p) d -> p k d", p=P), in_=zt[:])
 
         with tc.manual_schedule():
-            widen(('x', 0, 0), 3)
-            group(('x', 0, 0), nc.vector)
-            group(('g', 0, 0), nc.scalar)
-            widen(('x', 1, 0), 3)
-            quant(('x', 0, 0))
-            widen(('x', 2, 0), 0)
-            group(('g', 1, 0), nc.vector)
-            quant(('g', 0, 0))
-            group(('g', 2, 0), nc.scalar)
-            group(('x', 1, 0), nc.vector)
-            widen(('x', 3, 0), 2)
-            quant(('g', 1, 0))
-            group(('x', 2, 0), nc.vector)
-            widen(('x', 0, 1), 4)
-            quant(('g', 2, 0))
-            quant(('x', 2, 0))
-            widen(('x', 2, 1), 2)
-            widen(('x', 3, 1), 3)
-            group(('x', 3, 0), nc.vector)
-            group(('g', 3, 0), nc.scalar)
-            group(('g', 1, 1), nc.scalar)
-            group(('g', 3, 1), nc.scalar)
-            quant(('x', 1, 0))
-            group(('g', 0, 1), nc.vector)
-            quant(('x', 3, 0))
-            quant(('g', 3, 0))
-            group(('g', 2, 1), nc.scalar)
-            quant(('g', 1, 1))
-            widen(('x', 1, 1), 0)
-            group(('x', 3, 1), nc.vector)
-            c_mm(0, 0)
-            quant(('g', 0, 1))
-            group(('x', 2, 1), nc.vector)
-            quant(('g', 3, 1))
-            widen(('a', 0, 1), 0)
-            group(('x', 0, 1), nc.vector)
-            widen(('a', 1, 0), 0)
-            quant(('g', 2, 1))
-            quant(('x', 3, 1))
-            quant(('x', 2, 1))
-            c_out(0, 0, 0)
-            group(('x', 1, 1), nc.vector)
-            quant(('x', 0, 1))
-            quant(('x', 1, 1))
-            c_out(0, 0, 1)
-            c_mm(0, 1)
-            widen(('a', 0, 0), 1)
+            make_diag(0)
+            make_diag(1)
+            widen(("x", 0, 0), range(2, 4), True)
+            widen(("x", 0, 0), range(2), False)
+            group(("x", 0, 0), False)
+            widen(("x", 1, 0), range(2), False)
+            group(("g", 0, 0), True)
+            quant(("x", 0, 0))
+            group(("g", 1, 0), False)
+            widen(("x", 1, 0), range(2, 4), True)
+            quant(("g", 0, 0))
+            group(("x", 1, 0), False)
+            widen(("x", 2, 0), range(0, 4), True)
+            widen(("x", 3, 0), range(0, 4), True)
+            group(("g", 2, 0), False)
+            quant(("g", 1, 0))
+            quant(("g", 2, 0))
+            group(("x", 2, 0), False)
+            group(("g", 3, 0), False)
+            widen(("x", 2, 1), range(4), False)
+            quant(("x", 1, 0))
+            quant(("g", 3, 0))
+            group(("x", 3, 0), False)
+            widen(("x", 0, 1), range(0, 4), True)
+            quant(("x", 2, 0))
+            quant(("x", 3, 0))
+            widen(("x", 1, 1), range(0, 4), True)
+            group(("g", 0, 1), True)
+            group(("g", 1, 1), True)
+            group(("x", 0, 1), False)
+            group(("g", 2, 1), True)
+            quant(("g", 0, 1))
+            group(("x", 2, 1), False)
+            c_mm(0, 0, 1)
+            c_mm(0, 0, 0)
+            widen(("x", 3, 1), range(0, 4), True)
+            widen(("a", 3, 0), range(1, 4), True)
+            group(("g", 3, 1), False)
+            quant(("g", 1, 1))
+            quant(("g", 3, 1))
+            quant(("g", 2, 1))
+            group(("x", 1, 1), False)
+            widen(("a", 1, 0), range(0, 4), True)
+            quant(("x", 2, 1))
+            c_mm(0, 1, 0)
+            widen(("a", 3, 1), range(0, 4), True)
+            group(("x", 3, 1), False)
+            quant(("x", 0, 1))
+            quant(("x", 3, 1))
             c_out(0, 1, 0)
-            r_quant(0, 0)
-            group(('a', 0, 1), nc.vector)
-            group(('a', 1, 0), nc.vector)
-            group(('a', 0, 0), nc.vector)
-            widen(('a', 1, 1), 1)
+            quant(("x", 1, 1))
+            c_out(0, 0, 1)
+            c_mm(0, 1, 1)
+            c_mm(1, 0, 0)
+            group(("a", 3, 1), False)
             c_out(0, 1, 1)
-            quant(('a', 0, 0))
-            c_mm(1, 0)
-            quant(('a', 1, 0))
-            c_mm(1, 1)
-            group(('a', 1, 1), nc.vector)
-            widen(('a', 3, 0), 0)
-            quant(('a', 0, 1))
+            c_out(0, 0, 0)
+            c_mm(1, 1, 0)
+            widen(("a", 3, 0), range(1), False)
+            widen(("a", 1, 1), range(0, 4), True)
+            quant(("a", 3, 1))
+            c_mm(1, 0, 1)
+            c_mm(1, 1, 1)
             r_quant(0, 1)
-            c_out(1, 0, 0)
+            widen(("a", 0, 0), range(0, 4), True)
+            r_quant(0, 0)
+            group(("a", 3, 0), False)
+            group(("a", 1, 0), False)
+            group(("a", 1, 1), False)
             c_out(1, 1, 0)
-            quant(('a', 1, 1))
+            c_out(1, 0, 0)
+            quant(("a", 1, 1))
+            quant(("a", 3, 0))
+            quant(("a", 1, 0))
             c_out(1, 0, 1)
             c_out(1, 1, 1)
+            widen(("a", 0, 1), range(0, 4), True)
             r_quant(1, 0)
+            z_mm(0, 3, 1)
+            z_mm(0, 1, 0)
             r_quant(1, 1)
-            widen(('a', 2, 1), 2)
-            z_mm(0, 0)
-            z_mm(0, 1)
-            z_out(0, 0, 0, 0)
-            z_out(0, 0, 1, 0)
-            widen(('a', 2, 0), 4)
-            group(('a', 2, 1), nc.vector)
-            group(('a', 2, 0), nc.vector)
+            z_out(0, 3, 1, 0)
+            group(("a", 0, 1), False)
+            z_mm(0, 1, 1)
             z_out(0, 1, 0, 0)
-            quant(('a', 2, 1))
+            group(("a", 0, 0), False)
+            quant(("a", 0, 1))
             z_out(0, 1, 1, 0)
-            z_mm(1, 0)
-            z_mm(1, 1)
-            z_out(1, 0, 0, 0)
-            z_out(1, 0, 1, 0)
-            z_out(1, 1, 0, 0)
+            quant(("a", 0, 0))
+            widen(("a", 2, 1), range(4), False)
+            z_mm(1, 3, 1)
+            widen(("a", 2, 0), range(4), False)
+            z_mm(1, 1, 1)
+            z_mm(1, 1, 0)
+            group(("a", 2, 1), False)
+            z_out(1, 3, 1, 0)
+            z_mm(0, 0, 1)
             z_out(1, 1, 1, 0)
-            quant(('a', 2, 0))
-            widen(('a', 3, 1), 4)
-            group(('a', 3, 0), nc.vector)
-            z_mm(0, 2)
+            z_out(1, 1, 0, 0)
+            z_out(0, 0, 1, 0)
+            group(("a", 2, 0), False)
+            z_mm(1, 3, 0)
+            quant(("a", 2, 1))
+            quant(("a", 2, 0))
+            z_mm(1, 0, 0)
+            z_out(1, 3, 0, 0)
+            z_mm(1, 0, 1)
+            z_mm(0, 3, 0)
+            z_out(1, 0, 0, 0)
+            widen(("a", 4, 1), range(4), False)
+            z_out(1, 0, 1, 0)
+            z_out(0, 3, 0, 0)
+            widen(("a", 4, 0), range(4), False)
+            z_mm(0, 0, 0)
+            z_mm(1, 2, 0)
+            z_mm(0, 2, 0)
+            group(("a", 4, 1), False)
+            group(("a", 4, 0), False)
+            z_out(0, 0, 0, 0)
+            z_out(1, 2, 0, 0)
+            quant(("a", 4, 1))
+            quant(("a", 4, 0))
+            z_mm(0, 2, 1)
+            z_mm(1, 4, 1)
+            z_mm(0, 4, 0)
             z_out(0, 2, 0, 0)
             z_out(0, 2, 1, 0)
-            group(('a', 3, 1), nc.vector)
-            z_mm(1, 2)
-            quant(('a', 3, 0))
-            z_out(1, 2, 0, 0)
-            z_out(1, 2, 1, 0)
-            quant(('a', 3, 1))
-            z_mm(0, 3)
-            z_out(0, 3, 1, 0)
-            z_out(0, 3, 0, 2)
-            z_mm(1, 3)
-            z_out(1, 3, 0, 2)
-            z_out(1, 3, 1, 2)
+            z_out(1, 4, 1, 1)
+            z_mm(1, 2, 1)
+            z_out(0, 4, 0, 1)
+            z_mm(0, 4, 1)
+            z_mm(1, 4, 0)
+            z_out(1, 2, 1, 1)
+            z_out(0, 4, 1, 0)
+            z_out(1, 4, 0, 0)

@@ -21,7 +21,7 @@ W = 512
 KP = 512
 CP = T // KP
 GP = M // KP
-A_COLS = ((0, 512), (512, 512), (1024, 512), (1536, 256), (1792, 256))
+A_COLS = ((0, 512), (512, 512), (1024, 512), (1536, 512))
 
 
 def tile_loaded_microphone_covariance_d5_kernel(tc, X_bytes, X_scale, G, load, A_bytes, A_scale, out):
@@ -31,10 +31,10 @@ def tile_loaded_microphone_covariance_d5_kernel(tc, X_bytes, X_scale, G, load, A
         stage = ctx.enter_context(tc.tile_pool(name="stage", bufs=1))
         psum = ctx.enter_context(tc.psum_pool(name="psum", bufs=8))
 
-        lb = keep.tile([P, GP, 4], BF16, name="lb")
-        nc.scalar.dma_start(out=lb[:], in_=load.rearrange("(g p t) -> p g t", p=P, t=4))
         xsc = keep.tile([P, CP, 4], F32, name="xsc")
         nc.scalar.dma_start(out=xsc[:], in_=X_scale.rearrange("(c p t) o -> p c (t o)", p=P, t=4))
+        lb = keep.tile([P, GP, 4], BF16, name="lb")
+        nc.scalar.dma_start(out=lb[:], in_=load.rearrange("(g p t) -> p g t", p=P, t=4))
         asc = keep.tile([P, GP, 4], F32, name="asc")
         nc.scalar.dma_start(out=asc[:], in_=A_scale.rearrange("(g p t) o -> p g (t o)", p=P, t=4))
 
@@ -69,15 +69,26 @@ def tile_loaded_microphone_covariance_d5_kernel(tc, X_bytes, X_scale, G, load, A
 
         ident = keep.tile([P, P], BF16, name="ident")
         make_identity(nc, ident[:])
-        diag = {}
+        diag = keep.tile([P, GP, W, 4], BF16, name="diag")
+        eye = keep.tile([P, 4, 4], BF16, name="eye")
+        mask = keep.tile([P, P, 16], BF16, name="mask")
 
-        def make_diag(g):
-            diag[g] = keep.tile([P, W, 4], BF16, name="diag%d" % g)
-            nc.vector.memset(diag[g][:], 0.0)
+        def make_mask():
+            flat = eye[:].rearrange("p a t -> p (a t)")
+            nc.vector.memset(flat, 0.0)
+            nc.vector.memset(flat[:, 0:16:5], 1.0)
             nc.vector.tensor_tensor(
-                out=diag[g][:].rearrange("p (q a) t -> p q (a t)", a=4)[:, :, 0:16:5],
-                in0=ident[:].unsqueeze(2).to_broadcast([P, P, 4]),
-                in1=lb[:, g : g + 1, :].to_broadcast([P, P, 4]),
+                out=mask[:],
+                in0=ident[:].unsqueeze(2).to_broadcast([P, P, 16]),
+                in1=flat.unsqueeze(1).to_broadcast([P, P, 16]),
+                op=MULT,
+            )
+
+        def fill_diag(g):
+            nc.vector.tensor_tensor(
+                out=diag[:, g],
+                in0=mask[:].rearrange("p q (a t) -> p (q a) t", t=4),
+                in1=lb[:, g : g + 1, :].to_broadcast([P, W, 4]),
                 op=MULT,
             )
 
@@ -112,9 +123,16 @@ def tile_loaded_microphone_covariance_d5_kernel(tc, X_bytes, X_scale, G, load, A
                 else:
                     nc.vector.tensor_scalar(out=dst, in0=src, scalar1=sc[:, t : t + 1], scalar2=None, op0=MULT)
 
+        def pair_of(u):
+            if u[0] == "a":
+                return ("a", u[1], 0), u[2]
+            return (u[0], u[1] // 2, u[2]), u[1] % 2
+
         def group(u, on_scalar):
-            grouped[u] = stage.tile([P, 4 * width_of(u)], BF16, name="grouped", align_bytes=64, bufs=6)
-            gt = grouped[u][:]
+            pair, k = pair_of(u)
+            if pair not in grouped:
+                grouped[pair] = stage.tile([P, 2, 4 * width_of(u)], BF16, name="grouped", align_bytes=64, bufs=5)
+            gt = grouped[pair][:, k]
             if u[0] == "g":
                 dst = gt.rearrange("p (t m j) -> p m j t", t=4, j=4)
                 src = g_raw[u[1], u[2]][:].rearrange("p j (m t) -> p m j t", t=4)
@@ -132,7 +150,12 @@ def tile_loaded_microphone_covariance_d5_kernel(tc, X_bytes, X_scale, G, load, A
             nc.vector.quantize_mx(out=q[:].bitcast(FP8X4), scales=s[:], in_=src)
 
         def quant(u):
-            quantize(u, grouped[u][:], width_of(u))
+            pair, k = pair_of(u)
+            quantize(pair, grouped[pair][:].rearrange("p k w -> p (k w)"), 2 * width_of(u))
+
+        def part(u):
+            pair, k = pair_of(u)
+            return coded[pair], k * width_of(u)
 
         def mx(acc, left, lcol, right, rcol, n, first, last):
             nc.tensor.matmul_mx(
@@ -151,23 +174,25 @@ def tile_loaded_microphone_covariance_d5_kernel(tc, X_bytes, X_scale, G, load, A
                 bank["c", h, g, b] = acc
                 for t in range(4):
                     for c in range(CP):
-                        mx(acc[:, t], coded["g", c, g], P * t, coded["x", c, h], P * b, P, c == 0, c == CP - 1)
+                        gc, g0 = part(("g", c, g))
+                        xc, x0 = part(("x", c, h))
+                        mx(acc[:, t], gc, g0 + P * t, xc, x0 + P * b, P, c == 0, c == CP - 1)
 
         def c_out(h, g, half):
-            if (h, g) not in rows:
-                rows[h, g] = stage.tile([P, W, 4], BF16, name="rows", align_bytes=64, bufs=3)
+            if h not in rows:
+                rows[h] = stage.tile([P, GP, W, 4], BF16, name="rows", align_bytes=64, bufs=2)
             for b in (2 * half, 2 * half + 1):
                 src = bank["c", h, g, b][:].rearrange("p t i -> p i t")
-                dst = rows[h, g][:, P * b : P * (b + 1)]
+                dst = rows[h][:, g, P * b : P * (b + 1)]
                 if h == g:
                     nc.vector.scalar_tensor_tensor(
-                        out=dst, in0=src, scalar=1.0 / T, in1=diag[g][:, P * b : P * (b + 1)], op0=MULT, op1=ADD
+                        out=dst, in0=src, scalar=1.0 / T, in1=diag[:, g, P * b : P * (b + 1)], op0=MULT, op1=ADD
                     )
                 else:
                     nc.scalar.activation(out=dst, in_=src, func=COPY, scale=1.0 / T)
 
-        def r_quant(h, g):
-            quantize(("r", h, g), rows[h, g][:].rearrange("p w t -> p (w t)"), W)
+        def r_quant(h):
+            quantize(("r", h, 0), rows[h][:].rearrange("p g w t -> p (g w t)"), GP * W)
 
         def z_mm(h, d, half):
             w = A_COLS[d][1]
@@ -175,153 +200,128 @@ def tile_loaded_microphone_covariance_d5_kernel(tc, X_bytes, X_scale, G, load, A
                 acc = psum.tile([P, w], F32, name="bank")
                 bank["z", h, d, b] = acc
                 for g in range(GP):
-                    mx(acc[:], coded["r", h, g], P * b, coded["a", d, g], 0, w, g == 0, g == GP - 1)
+                    ac, a0 = part(("a", d, g))
+                    mx(acc[:], coded["r", h, 0], W * g + P * b, ac, a0, w, g == 0, g == GP - 1)
 
         def z_out(h, d, half, on_vector):
             lo, w = A_COLS[d]
-            zt = stage.tile([P, 2, w], F32, name="zt", tag="stream", bufs=8)
             for k in range(2):
-                src = bank["z", h, d, 2 * half + k]
+                b = 2 * half + k
+                zt = stage.tile([P, w], F32, name="zt", tag="stream", bufs=8)
                 if k < on_vector:
-                    nc.vector.tensor_copy(out=zt[:, k], in_=src[:])
+                    nc.vector.tensor_copy(out=zt[:], in_=bank["z", h, d, b][:])
                 else:
-                    nc.scalar.copy(out=zt[:, k], in_=src[:])
-            row = W * h + 2 * P * half
-            nc.sync.dma_start(out=out[row : row + 2 * P, lo : lo + w].rearrange("(k p) d -> p k d", p=P), in_=zt[:])
+                    nc.scalar.copy(out=zt[:], in_=bank["z", h, d, b][:])
+                row = W * h + P * b
+                nc.sync.dma_start(out=out[row : row + P, lo : lo + w], in_=zt[:])
 
         with tc.manual_schedule():
-            make_diag(0)
-            make_diag(1)
-            widen(("x", 0, 0), range(2, 4), True)
-            widen(("x", 0, 0), range(2), False)
-            group(("x", 0, 0), False)
-            widen(("x", 1, 0), range(2), False)
+            make_mask()
+            widen(("x", 0, 0), range(1, 4), True)
+            widen(("x", 0, 0), range(1), False)
+            fill_diag(1)
             group(("g", 0, 0), True)
-            quant(("x", 0, 0))
-            group(("g", 1, 0), False)
-            widen(("x", 1, 0), range(2, 4), True)
-            quant(("g", 0, 0))
+            fill_diag(0)
+            widen(("x", 1, 0), range(4), False)
+            group(("x", 0, 0), False)
+            widen(("x", 2, 0), range(3), False)
+            group(("g", 1, 0), True)
+            widen(("x", 2, 0), range(3, 4), True)
             group(("x", 1, 0), False)
-            widen(("x", 2, 0), range(0, 4), True)
+            quant(("g", 0, 0))
+            quant(("x", 0, 0))
+            group(("x", 2, 0), False)
             widen(("x", 3, 0), range(0, 4), True)
             group(("g", 2, 0), False)
-            quant(("g", 1, 0))
-            quant(("g", 2, 0))
-            group(("x", 2, 0), False)
-            group(("g", 3, 0), False)
-            widen(("x", 2, 1), range(4), False)
-            quant(("x", 1, 0))
-            quant(("g", 3, 0))
+            widen(("x", 2, 1), range(3), False)
+            widen(("x", 3, 1), range(4), False)
             group(("x", 3, 0), False)
             widen(("x", 0, 1), range(0, 4), True)
-            quant(("x", 2, 0))
-            quant(("x", 3, 0))
-            widen(("x", 1, 1), range(0, 4), True)
+            group(("g", 3, 0), True)
+            widen(("x", 2, 1), range(3, 4), True)
             group(("g", 0, 1), True)
-            group(("g", 1, 1), True)
-            group(("x", 0, 1), False)
+            quant(("g", 2, 0))
+            quant(("x", 2, 0))
             group(("g", 2, 1), True)
+            c_mm(0, 0, 0)
+            group(("g", 3, 1), True)
+            group(("g", 1, 1), False)
+            widen(("x", 1, 1), range(0, 4), True)
+            c_mm(0, 0, 1)
+            group(("x", 3, 1), False)
             quant(("g", 0, 1))
             group(("x", 2, 1), False)
-            c_mm(0, 0, 1)
-            c_mm(0, 0, 0)
-            widen(("x", 3, 1), range(0, 4), True)
-            widen(("a", 3, 0), range(1, 4), True)
-            group(("g", 3, 1), False)
-            quant(("g", 1, 1))
-            quant(("g", 3, 1))
             quant(("g", 2, 1))
-            group(("x", 1, 1), False)
             widen(("a", 1, 0), range(0, 4), True)
-            quant(("x", 2, 1))
-            c_mm(0, 1, 0)
-            widen(("a", 3, 1), range(0, 4), True)
-            group(("x", 3, 1), False)
-            quant(("x", 0, 1))
-            quant(("x", 3, 1))
-            c_out(0, 1, 0)
-            quant(("x", 1, 1))
-            c_out(0, 0, 1)
+            group(("x", 0, 1), False)
+            group(("x", 1, 1), False)
             c_mm(0, 1, 1)
-            c_mm(1, 0, 0)
-            group(("a", 3, 1), False)
-            c_out(0, 1, 1)
-            c_out(0, 0, 0)
-            c_mm(1, 1, 0)
-            widen(("a", 3, 0), range(1), False)
-            widen(("a", 1, 1), range(0, 4), True)
-            quant(("a", 3, 1))
-            c_mm(1, 0, 1)
-            c_mm(1, 1, 1)
-            r_quant(0, 1)
+            c_mm(0, 1, 0)
             widen(("a", 0, 0), range(0, 4), True)
-            r_quant(0, 0)
-            group(("a", 3, 0), False)
+            c_out(0, 1, 0)
+            quant(("x", 2, 1))
+            quant(("x", 0, 1))
+            widen(("a", 2, 0), range(3, 4), True)
+            widen(("a", 1, 1), range(0, 4), True)
+            c_out(0, 0, 0)
+            c_mm(1, 1, 1)
+            c_out(0, 1, 1)
+            c_out(0, 0, 1)
             group(("a", 1, 0), False)
-            group(("a", 1, 1), False)
-            c_out(1, 1, 0)
-            c_out(1, 0, 0)
-            quant(("a", 1, 1))
-            quant(("a", 3, 0))
-            quant(("a", 1, 0))
-            c_out(1, 0, 1)
-            c_out(1, 1, 1)
-            widen(("a", 0, 1), range(0, 4), True)
-            r_quant(1, 0)
-            z_mm(0, 3, 1)
-            z_mm(0, 1, 0)
-            r_quant(1, 1)
-            z_out(0, 3, 1, 0)
-            group(("a", 0, 1), False)
-            z_mm(0, 1, 1)
-            z_out(0, 1, 0, 0)
             group(("a", 0, 0), False)
-            quant(("a", 0, 1))
-            z_out(0, 1, 1, 0)
+            widen(("a", 0, 1), range(0, 4), True)
+            c_mm(1, 0, 0)
+            c_out(1, 1, 1)
+            group(("a", 1, 1), False)
+            widen(("a", 3, 0), range(0, 4), True)
+            r_quant(0)
+            c_out(1, 0, 0)
+            c_mm(1, 0, 1)
+            c_mm(1, 1, 0)
+            c_out(1, 0, 1)
+            quant(("a", 1, 0))
+            z_mm(0, 1, 0)
+            group(("a", 0, 1), False)
+            c_out(1, 1, 0)
             quant(("a", 0, 0))
-            widen(("a", 2, 1), range(4), False)
-            z_mm(1, 3, 1)
-            widen(("a", 2, 0), range(4), False)
-            z_mm(1, 1, 1)
-            z_mm(1, 1, 0)
-            group(("a", 2, 1), False)
-            z_out(1, 3, 1, 0)
+            z_out(0, 1, 0, 0)
+            z_mm(0, 1, 1)
             z_mm(0, 0, 1)
-            z_out(1, 1, 1, 0)
-            z_out(1, 1, 0, 0)
+            r_quant(1)
+            z_out(0, 1, 1, 0)
+            widen(("a", 3, 1), range(4), False)
             z_out(0, 0, 1, 0)
+            group(("a", 3, 0), False)
+            z_mm(1, 1, 0)
+            group(("a", 3, 1), False)
+            z_mm(0, 0, 0)
+            z_mm(1, 0, 1)
+            widen(("a", 2, 0), range(3), False)
+            z_mm(1, 0, 0)
+            z_out(1, 1, 0, 0)
+            quant(("a", 3, 0))
+            z_mm(1, 1, 1)
+            z_out(0, 0, 0, 0)
+            z_mm(0, 3, 0)
+            z_out(1, 0, 1, 0)
+            z_out(1, 0, 0, 0)
+            z_mm(0, 3, 1)
+            z_out(1, 1, 1, 0)
+            widen(("a", 2, 1), range(4), False)
             group(("a", 2, 0), False)
             z_mm(1, 3, 0)
-            quant(("a", 2, 1))
-            quant(("a", 2, 0))
-            z_mm(1, 0, 0)
-            z_out(1, 3, 0, 0)
-            z_mm(1, 0, 1)
-            z_mm(0, 3, 0)
-            z_out(1, 0, 0, 0)
-            widen(("a", 4, 1), range(4), False)
-            z_out(1, 0, 1, 0)
+            z_mm(1, 3, 1)
             z_out(0, 3, 0, 0)
-            widen(("a", 4, 0), range(4), False)
-            z_mm(0, 0, 0)
-            z_mm(1, 2, 0)
-            z_mm(0, 2, 0)
-            group(("a", 4, 1), False)
-            group(("a", 4, 0), False)
-            z_out(0, 0, 0, 0)
-            z_out(1, 2, 0, 0)
-            quant(("a", 4, 1))
-            quant(("a", 4, 0))
-            z_mm(0, 2, 1)
-            z_mm(1, 4, 1)
-            z_mm(0, 4, 0)
-            z_out(0, 2, 0, 0)
-            z_out(0, 2, 1, 0)
-            z_out(1, 4, 1, 1)
+            z_out(0, 3, 1, 0)
+            z_out(1, 3, 0, 0)
+            group(("a", 2, 1), False)
+            quant(("a", 2, 0))
             z_mm(1, 2, 1)
-            z_out(0, 4, 0, 1)
-            z_mm(0, 4, 1)
-            z_mm(1, 4, 0)
+            z_out(1, 3, 1, 0)
+            z_mm(1, 2, 0)
             z_out(1, 2, 1, 1)
-            z_out(0, 4, 1, 0)
-            z_out(1, 4, 0, 0)
+            z_mm(0, 2, 1)
+            z_out(1, 2, 0, 1)
+            z_mm(0, 2, 0)
+            z_out(0, 2, 1, 1)
+            z_out(0, 2, 0, 2)

from contextlib import ExitStack

import concourse.mybir as mybir
from concourse.masks import make_identity

T, M, D = 2048, 1024, 2048
FLOPS = 2 * T * M * M + 2 * M * M * D

F32 = mybir.dt.float32
BF16 = mybir.dt.bfloat16
U32 = mybir.dt.uint32
U8 = mybir.dt.uint8
FP8 = mybir.dt.float8_e4m3fn
FP8X4 = mybir.dt.float8_e4m3fn_x4
COPY = mybir.ActivationFunctionType.Copy
MULT = mybir.AluOpType.mult
ADD = mybir.AluOpType.add

P = 128
W = 512
KP = 512
CP = T // KP
GP = M // KP
A_COLS = ((0, 512), (512, 512), (1024, 512), (1536, 512))


def tile_loaded_microphone_covariance_d5_kernel(tc, X_bytes, X_scale, G, load, A_bytes, A_scale, out):
    nc = tc.nc
    with ExitStack() as ctx:
        keep = ctx.enter_context(tc.tile_pool(name="keep", bufs=1))
        stage = ctx.enter_context(tc.tile_pool(name="stage", bufs=1))
        psum = ctx.enter_context(tc.psum_pool(name="psum", bufs=8))

        xsc = keep.tile([P, CP, 4], F32, name="xsc")
        nc.scalar.dma_start(out=xsc[:], in_=X_scale.rearrange("(c p t) o -> p c (t o)", p=P, t=4))
        lb = keep.tile([P, GP, 4], BF16, name="lb")
        nc.scalar.dma_start(out=lb[:], in_=load.rearrange("(g p t) -> p g t", p=P, t=4))
        asc = keep.tile([P, GP, 4], F32, name="asc")
        nc.scalar.dma_start(out=asc[:], in_=A_scale.rearrange("(g p t) o -> p g (t o)", p=P, t=4))

        xv = X_bytes.rearrange("(c p t) w -> c p t w", p=P, t=4)
        gv = G.rearrange("(c p t) w -> c p t w", p=P, t=4)
        av = A_bytes.rearrange("(g p t) w -> g p t w", p=P, t=4)
        x_raw = {}
        g_raw = {}
        a_raw = {}

        def load_x(c, h):
            x_raw[c, h] = keep.tile([P, 4, W], U8, name="xraw%d%d" % (c, h))
            cuts = (0, 2, 4) if c == 0 and h == 0 else (0, 4)
            for lo, hi in zip(cuts, cuts[1:]):
                nc.sync.dma_start(out=x_raw[c, h][:, lo:hi], in_=xv[c][:, lo:hi, W * h : W * (h + 1)])

        def load_g(c, h):
            g_raw[c, h] = stage.tile([P, 4, W], BF16, name="graw%d%d" % (c, h), tag="stream", bufs=8)
            nc.sync.dma_start(out=g_raw[c, h][:], in_=gv[c][:, :, W * h : W * (h + 1)])

        for c in range(CP):
            load_x(c, 0)
            load_g(c, 0)
        for c in range(CP):
            load_x(c, 1)
        for c in range(CP):
            load_g(c, 1)
        for h in range(2):
            for g in range(GP):
                a_raw[g, h] = keep.tile([P, 4, 1024], U8, name="araw%d%d" % (g, h))
                nc.sync.dma_start(out=a_raw[g, h][:], in_=av[g][:, :, 1024 * h : 1024 * (h + 1)])

        ident = keep.tile([P, P], BF16, name="ident")
        make_identity(nc, ident[:])
        diag = keep.tile([P, GP, W, 4], BF16, name="diag")
        eye = keep.tile([P, 4, 4], BF16, name="eye")
        mask = keep.tile([P, P, 16], BF16, name="mask")

        def make_mask():
            flat = eye[:].rearrange("p a t -> p (a t)")
            nc.vector.memset(flat, 0.0)
            nc.vector.memset(flat[:, 0:16:5], 1.0)
            nc.vector.tensor_tensor(
                out=mask[:],
                in0=ident[:].unsqueeze(2).to_broadcast([P, P, 16]),
                in1=flat.unsqueeze(1).to_broadcast([P, P, 16]),
                op=MULT,
            )

        def fill_diag(g):
            nc.vector.tensor_tensor(
                out=diag[:, g],
                in0=mask[:].rearrange("p q (a t) -> p (q a) t", t=4),
                in1=lb[:, g : g + 1, :].to_broadcast([P, W, 4]),
                op=MULT,
            )

        def codes(name, width):
            q = keep.tile([P, width], U32, name=name + "q", align_bytes=64)
            s = keep.tile([P, width], U8, name=name + "s", align_bytes=64)
            return q, s

        wide = {}
        grouped = {}
        coded = {}
        bank = {}
        rows = {}

        def width_of(u):
            return A_COLS[u[1]][1] if u[0] == "a" else W

        def bytes_of(u):
            if u[0] == "x":
                return x_raw[u[1], u[2]][:], xsc[:, u[1]]
            lo, w = A_COLS[u[1]]
            return a_raw[u[2], lo // 1024][:, :, lo % 1024 : lo % 1024 + w], asc[:, u[2]]

        def widen(u, planes, on_scalar):
            raw, sc = bytes_of(u)
            if u not in wide:
                wide[u] = stage.tile([P, 4, width_of(u)], BF16, name="wide", align_bytes=64, bufs=6)
            for t in planes:
                dst, src = wide[u][:, t], raw[:, t].bitcast(FP8)
                if on_scalar:
                    nc.scalar.activation(out=dst, in_=src, func=COPY, scale=sc[:, t : t + 1])
                else:
                    nc.vector.tensor_scalar(out=dst, in0=src, scalar1=sc[:, t : t + 1], scalar2=None, op0=MULT)

        def pair_of(u):
            if u[0] == "a":
                return ("a", u[1], 0), u[2]
            return (u[0], u[1] // 2, u[2]), u[1] % 2

        def group(u, on_scalar):
            pair, k = pair_of(u)
            if pair not in grouped:
                grouped[pair] = stage.tile([P, 2, 4 * width_of(u)], BF16, name="grouped", align_bytes=64, bufs=5)
            gt = grouped[pair][:, k]
            if u[0] == "g":
                dst = gt.rearrange("p (t m j) -> p m j t", t=4, j=4)
                src = g_raw[u[1], u[2]][:].rearrange("p j (m t) -> p m j t", t=4)
            else:
                dst = gt.rearrange("p (c i t) -> p c t i", i=4, t=4)
                src = wide[u][:].rearrange("p t (c i) -> p c t i", i=4)
            if on_scalar:
                nc.scalar.copy(out=dst, in_=src)
            else:
                nc.vector.tensor_copy(out=dst, in_=src)

        def quantize(key, src, width):
            q, s = codes("%s%d%d" % key, width)
            coded[key] = q, s
            nc.vector.quantize_mx(out=q[:].bitcast(FP8X4), scales=s[:], in_=src)

        def quant(u):
            pair, k = pair_of(u)
            quantize(pair, grouped[pair][:].rearrange("p k w -> p (k w)"), 2 * width_of(u))

        def part(u):
            pair, k = pair_of(u)
            return coded[pair], k * width_of(u)

        def mx(acc, left, lcol, right, rcol, n, first, last):
            nc.tensor.matmul_mx(
                out=acc,
                lhsT=left[0][:, lcol : lcol + P].bitcast(FP8X4),
                lhsT_scale=left[1][:, lcol : lcol + P],
                rhs=right[0][:, rcol : rcol + n].bitcast(FP8X4),
                rhs_scale=right[1][:, rcol : rcol + n],
                start=first,
                stop=last,
            )

        def c_mm(h, g, half):
            for b in (2 * half, 2 * half + 1):
                acc = psum.tile([P, 4, P], F32, name="bank")
                bank["c", h, g, b] = acc
                for t in range(4):
                    for c in range(CP):
                        gc, g0 = part(("g", c, g))
                        xc, x0 = part(("x", c, h))
                        mx(acc[:, t], gc, g0 + P * t, xc, x0 + P * b, P, c == 0, c == CP - 1)

        def c_out(h, g, half):
            if h not in rows:
                rows[h] = stage.tile([P, GP, W, 4], BF16, name="rows", align_bytes=64, bufs=2)
            for b in (2 * half, 2 * half + 1):
                src = bank["c", h, g, b][:].rearrange("p t i -> p i t")
                dst = rows[h][:, g, P * b : P * (b + 1)]
                if h == g:
                    nc.vector.scalar_tensor_tensor(
                        out=dst, in0=src, scalar=1.0 / T, in1=diag[:, g, P * b : P * (b + 1)], op0=MULT, op1=ADD
                    )
                else:
                    nc.scalar.activation(out=dst, in_=src, func=COPY, scale=1.0 / T)

        def r_quant(h):
            quantize(("r", h, 0), rows[h][:].rearrange("p g w t -> p (g w t)"), GP * W)

        def z_mm(h, d, half):
            w = A_COLS[d][1]
            for b in (2 * half, 2 * half + 1):
                acc = psum.tile([P, w], F32, name="bank")
                bank["z", h, d, b] = acc
                for g in range(GP):
                    ac, a0 = part(("a", d, g))
                    mx(acc[:], coded["r", h, 0], W * g + P * b, ac, a0, w, g == 0, g == GP - 1)

        def z_out(h, d, half, on_vector):
            lo, w = A_COLS[d]
            for k in range(2):
                b = 2 * half + k
                zt = stage.tile([P, w], F32, name="zt", tag="stream", bufs=8)
                if k < on_vector:
                    nc.vector.tensor_copy(out=zt[:], in_=bank["z", h, d, b][:])
                else:
                    nc.scalar.copy(out=zt[:], in_=bank["z", h, d, b][:])
                row = W * h + P * b
                nc.sync.dma_start(out=out[row : row + P, lo : lo + w], in_=zt[:])

        with tc.manual_schedule():
            make_mask()
            widen(("x", 0, 0), range(1, 4), True)
            widen(("x", 0, 0), range(1), False)
            fill_diag(1)
            group(("g", 0, 0), True)
            fill_diag(0)
            widen(("x", 1, 0), range(4), False)
            group(("x", 0, 0), False)
            widen(("x", 2, 0), range(3), False)
            group(("g", 1, 0), True)
            widen(("x", 2, 0), range(3, 4), True)
            group(("x", 1, 0), False)
            quant(("g", 0, 0))
            quant(("x", 0, 0))
            group(("x", 2, 0), False)
            widen(("x", 3, 0), range(0, 4), True)
            group(("g", 2, 0), False)
            widen(("x", 2, 1), range(3), False)
            widen(("x", 3, 1), range(4), False)
            group(("x", 3, 0), False)
            widen(("x", 0, 1), range(0, 4), True)
            group(("g", 3, 0), True)
            widen(("x", 2, 1), range(3, 4), True)
            group(("g", 0, 1), True)
            quant(("g", 2, 0))
            quant(("x", 2, 0))
            group(("g", 2, 1), True)
            c_mm(0, 0, 0)
            group(("g", 3, 1), True)
            group(("g", 1, 1), False)
            widen(("x", 1, 1), range(0, 4), True)
            c_mm(0, 0, 1)
            group(("x", 3, 1), False)
            quant(("g", 0, 1))
            group(("x", 2, 1), False)
            quant(("g", 2, 1))
            widen(("a", 1, 0), range(0, 4), True)
            group(("x", 0, 1), False)
            group(("x", 1, 1), False)
            c_mm(0, 1, 1)
            c_mm(0, 1, 0)
            widen(("a", 0, 0), range(0, 4), True)
            c_out(0, 1, 0)
            quant(("x", 2, 1))
            quant(("x", 0, 1))
            widen(("a", 2, 0), range(3, 4), True)
            widen(("a", 1, 1), range(0, 4), True)
            c_out(0, 0, 0)
            c_mm(1, 1, 1)
            c_out(0, 1, 1)
            c_out(0, 0, 1)
            group(("a", 1, 0), False)
            group(("a", 0, 0), False)
            widen(("a", 0, 1), range(0, 4), True)
            c_mm(1, 0, 0)
            c_out(1, 1, 1)
            group(("a", 1, 1), False)
            widen(("a", 3, 0), range(0, 4), True)
            r_quant(0)
            c_out(1, 0, 0)
            c_mm(1, 0, 1)
            c_mm(1, 1, 0)
            c_out(1, 0, 1)
            quant(("a", 1, 0))
            z_mm(0, 1, 0)
            group(("a", 0, 1), False)
            c_out(1, 1, 0)
            quant(("a", 0, 0))
            z_out(0, 1, 0, 0)
            z_mm(0, 1, 1)
            z_mm(0, 0, 1)
            r_quant(1)
            z_out(0, 1, 1, 0)
            widen(("a", 3, 1), range(4), False)
            z_out(0, 0, 1, 0)
            group(("a", 3, 0), False)
            z_mm(1, 1, 0)
            group(("a", 3, 1), False)
            z_mm(0, 0, 0)
            z_mm(1, 0, 1)
            widen(("a", 2, 0), range(3), False)
            z_mm(1, 0, 0)
            z_out(1, 1, 0, 0)
            quant(("a", 3, 0))
            z_mm(1, 1, 1)
            z_out(0, 0, 0, 0)
            z_mm(0, 3, 0)
            z_out(1, 0, 1, 0)
            z_out(1, 0, 0, 0)
            z_mm(0, 3, 1)
            z_out(1, 1, 1, 0)
            widen(("a", 2, 1), range(4), False)
            group(("a", 2, 0), False)
            z_mm(1, 3, 0)
            z_mm(1, 3, 1)
            z_out(0, 3, 0, 0)
            z_out(0, 3, 1, 0)
            z_out(1, 3, 0, 0)
            group(("a", 2, 1), False)
            quant(("a", 2, 0))
            z_mm(1, 2, 1)
            z_out(1, 3, 1, 0)
            z_mm(1, 2, 0)
            z_out(1, 2, 1, 1)
            z_mm(0, 2, 1)
            z_out(1, 2, 0, 1)
            z_mm(0, 2, 0)
            z_out(0, 2, 1, 1)
            z_out(0, 2, 0, 2)
